import numpy as np
import ml_dtypes


def mxq(x, axis, fmt="e4m3"):
    dtype, down = {"e4m3": (ml_dtypes.float8_e4m3fn, 7), "e5m2": (ml_dtypes.float8_e5m2, 14)}[fmt]
    v = np.moveaxis(np.asarray(x, np.float32).astype(ml_dtypes.bfloat16).astype(np.float64), axis, -1)
    blocks = v.reshape(v.shape[:-1] + (-1, 32))
    amax = np.abs(blocks).max(-1, keepdims=True)
    byte = np.maximum(np.where(amax > 0, np.frexp(amax)[1] - 1 + 127, 0) - down, 1)
    scale = np.exp2(byte - 127.0)
    codes = (blocks / scale).astype(np.float32).astype(dtype).astype(np.float64)
    return np.moveaxis((codes * scale).reshape(v.shape), -1, axis)


WIDE = False


def mx_kscale(k):
    if not WIDE:
        return np.ones(k)
    levels = np.array([10, -10, 5, -5, 0])
    if k % 512:
        return np.exp2(np.random.permutation(np.resize(levels, k // 32))).repeat(32)
    a = np.empty((k // 512, 16))
    for p in range(k // 512):
        a[p, :8] = np.random.permutation(np.resize(levels, 8))
        for g in range(8):
            far = levels[np.abs(levels - a[p, g]) >= 10]
            a[p, g + 8] = far[np.random.randint(len(far))]
    return np.exp2(a.ravel()).repeat(32)


BF16 = ml_dtypes.bfloat16


def bf(x):
    return np.asarray(x, np.float32).astype(BF16)


def f64(x):
    return np.asarray(x).astype(np.float64)


P, A = 512, 2048

STRENGTH = 0.35


def setup_inputs():
    s, t = mx_kscale(P), mx_kscale(A)
    return {"v": bf(np.random.standard_normal((P, A)) * s[:, None] * t),
            "fac": bf(STRENGTH * np.random.standard_normal((P, P)) / np.sqrt(P) / s),
            "comp": bf(STRENGTH * np.random.standard_normal((A, A)) / np.sqrt(A) / t[:, None]),
            "stay": bf((1 + 0.1 * np.random.standard_normal(P)) / s),
            "loyal": bf((1 + 0.1 * np.random.standard_normal(A)) / t),
            "bloom": bf(np.random.uniform(0.5, 1.5, P) * s)}


def reference(v, fac, comp, stay, loyal, bloom):
    v = f64(v)
    fq = mxq(f64(fac), 1, "e4m3")
    cq = mxq(f64(comp), 0, "e4m3")
    a = f64(stay)[:, None] * v + (fq @ mxq(v, 0, "e4m3"))
    b = f64(loyal) * a - (mxq(a, 1, "e4m3") @ cq)
    h = f64(bloom)[:, None] * b
    return b + (fq @ mxq(h, 0, "e4m3"))

@@ -1,0 +1,345 @@
+from contextlib import ExitStack
+
+import concourse.mybir as mybir
+from concourse.masks import make_identity
+
+F32 = mybir.dt.float32
+BF16 = mybir.dt.bfloat16
+U32 = mybir.dt.uint32
+U8 = mybir.dt.uint8
+FP8X4 = mybir.dt.float8_e4m3fn_x4
+ADD = mybir.AluOpType.add
+SUB = mybir.AluOpType.subtract
+MULT = mybir.AluOpType.mult
+COPY = mybir.ActivationFunctionType.Copy
+
+PLANTS, POLLS = 512, 2048
+P = 128
+T = 4
+W = 512
+G = POLLS // W
+FLOPS = 2 * PLANTS * POLLS * (2 * PLANTS + POLLS)
+
+V_FIRST = 0
+H_ON_SCALAR = (0, 3)
+D_V = [0,0,0,0]
+IV = ["s","s","s","v"]
+IV_AT = [0,0,0,2]
+IC = [["v","v","v","s"],["s","s","s","s"],["s","s","s","s"],["s","s","s","s"]]
+IC_AT = [[4,7,8,4],[9,6,9,10],[12,12,13,12],[15,16,17,18]]
+D_BUFS = 1
+D0_AT = 1
+LOY = 3
+
+
+def tile_pollinator_visit_response_t1_kernel(tc, v, fac, comp, stay, loyal, bloom, out):
+    nc = tc.nc
+    with ExitStack() as ctx:
+        const = ctx.enter_context(tc.tile_pool(name="const", bufs=1))
+        raws = ctx.enter_context(tc.tile_pool(name="raws", bufs=9))
+        keep = ctx.enter_context(tc.tile_pool(name="keep", bufs=1))
+        work = ctx.enter_context(tc.tile_pool(name="work", bufs=4))
+        psum = ctx.enter_context(tc.psum_pool(name="psum", bufs=4))
+
+        ident = const.tile([P, P], F32, name="ident")
+        stay_sb = const.tile([P, T], BF16, name="stay_sb")
+        bloom_sb = const.tile([P, T], BF16, name="bloom_sb")
+        bloom_f = const.tile([P, T], F32, name="bloom_f")
+        loyal_sb = const.tile([P, POLLS], BF16, name="loyal_sb")
+        v_sb = [keep.tile([P, T, W], BF16, name="v_sb%d" % g) for g in range(G)]
+        fq = keep.tile([P, PLANTS], U32, name="fq", align_bytes=64)
+        fs = keep.tile([P, PLANTS], U8, name="fs", align_bytes=64)
+        aq = [keep.tile([P, PLANTS], U32, name="aq%d" % g, align_bytes=64) for g in range(G)]
+        as_ = [keep.tile([P, PLANTS], U8, name="as%d" % g, align_bytes=64) for g in range(G)]
+        d = {}
+
+        out_v = out.rearrange("(p t) w -> p t w", t=T)
+        vq, vs, vi, ai, a32, ps1, psT = {}, {}, {}, {}, {}, {}, {}
+        raw, ci, cq, cs = {}, {}, {}, {}
+        ps2, b, hb, hi, hq, hs, ps3 = {}, {}, {}, {}, {}, {}, {}
+
+        def cols(g):
+            return slice(g * W, (g + 1) * W)
+
+        def sub(u):
+            return slice(u * P, (u + 1) * P)
+
+        def load_v(g):
+            nc.sync.dma_start(out=v_sb[g][:], in_=v.rearrange("(p t) w -> p t w", t=T)[:, :, cols(g)])
+
+        def load_c(g, n):
+            raw[g, n] = raws.tile([P, T, W], BF16, name="raw", align_bytes=64)
+            nc.sync.dma_start(
+                out=raw[g, n][:],
+                in_=comp[g * W : (g + 1) * W, cols(n)].rearrange("(p t) w -> p t w", t=T),
+            )
+
+        def grouped(name):
+            return work.tile([P, W, T], BF16, name=name, align_bytes=64)
+
+        def interleave(eng, dst, src, lo, hi_):
+            o = dst[:, lo:hi_, :].rearrange("p (c i) t -> p c t i", i=4)
+            s = src[:, :, lo:hi_].rearrange("p t (c i) -> p c t i", i=4)
+            if eng == "v":
+                nc.vector.tensor_copy(out=o, in_=s)
+            elif eng == "s":
+                nc.scalar.copy(out=o, in_=s)
+            else:
+                nc.gpsimd.tensor_scalar(out=o, in0=s, scalar1=1.0, scalar2=0.0, op0=MULT, op1=ADD)
+
+        def quantize(codes, scales, src):
+            nc.vector.quantize_mx(
+                out=codes[:].bitcast(FP8X4), scales=scales[:], in_=src[:].rearrange("p w t -> p (w t)")
+            )
+
+        def mm(acc, lc, ls, lcols, rc, rs, start, stop):
+            nc.tensor.matmul_mx(
+                out=acc[:],
+                lhsT=lc[:, lcols].bitcast(FP8X4),
+                lhsT_scale=ls[:, lcols],
+                rhs=rc[:].bitcast(FP8X4),
+                rhs_scale=rs[:],
+                start=start,
+                stop=stop,
+            )
+
+        def I_v(g, eng, lo=0, hi_=W):
+            if g not in vi:
+                vi[g] = grouped("gA")
+            interleave(eng, vi[g], v_sb[g], lo, hi_)
+
+        def Q_v(g):
+            vq[g] = work.tile([P, W], U32, name="vq", align_bytes=64, bufs=2)
+            vs[g] = work.tile([P, W], U8, name="vs", align_bytes=64, bufs=2)
+            quantize(vq[g], vs[g], vi[g])
+
+        def M1(g, u):
+            ps1[g, u] = psum.tile([P, W], F32, name="x")
+            mm(ps1[g, u], fq, fs, sub(u), vq[g], vs[g], True, True)
+
+        def A(g, u):
+            if u == 0:
+                a32[g] = work.tile([P, T, W], F32, name="w32")
+            nc.vector.scalar_tensor_tensor(
+                out=a32[g][:, u, :].rearrange("p (t m) -> p t m", t=T),
+                in0=v_sb[g][:, u, :].rearrange("p (m t) -> p t m", t=T),
+                scalar=stay_sb[:, u : u + 1],
+                in1=ps1[g, u][:].rearrange("p (m t) -> p t m", t=T),
+                op0=MULT,
+                op1=ADD,
+            )
+
+        def TR(g, u):
+            psT[g, u] = psum.tile([P, T, P], F32, name="y")
+            for t in range(T):
+                nc.tensor.transpose(psT[g, u][:, t, :], a32[g][:, u, sub(t)], ident[:])
+
+        def C(g, u):
+            if u == 0:
+                ai[g] = grouped("gA")
+            nc.scalar.copy(
+                out=ai[g][:, sub(u), :], in_=psT[g, u][:].rearrange("p t m -> p m t")
+            )
+
+        def Q_a(g):
+            quantize(aq[g], as_[g], ai[g])
+
+        def D(g, u):
+            d[g, u] = work.tile([P, W], F32, name="d%d" % u, bufs=D_BUFS)
+            (nc.vector if D_V[g] else nc.gpsimd).tensor_tensor(
+                out=d[g, u][:].rearrange("p (m t) -> p m t", t=T),
+                in0=a32[g][:, u, :].rearrange("p (t m) -> p m t", t=T),
+                in1=loyal_sb[:, cols(g)].rearrange("p (m t) -> p m t", t=T),
+                op=MULT,
+            )
+
+        def I_c(g, n):
+            ci[g, n] = work.tile([P, W, T], BF16, name="ci", align_bytes=64, bufs=8)
+            interleave(IC[n][g], ci[g, n], raw[g, n], 0, W)
+
+        def Q_c(g, n):
+            cq[g, n] = work.tile([P, W], U32, name="cq", align_bytes=64, bufs=8)
+            cs[g, n] = work.tile([P, W], U8, name="cs", align_bytes=64, bufs=8)
+            quantize(cq[g, n], cs[g, n], ci[g, n])
+
+        def M2(n, u, g):
+            if g == 0:
+                ps2[n, u] = psum.tile([P, W], F32, name="x")
+            mm(ps2[n, u], aq[g], as_[g], sub(u), cq[g, n], cs[g, n], g == 0, g == G - 1)
+
+        def B(n, u):
+            if u == 0:
+                b[n] = work.tile([P, T, W], F32, name="w32")
+            nc.vector.tensor_tensor(out=b[n][:, u, :], in0=d[n, u][:], in1=ps2[n, u][:], op=SUB)
+
+        def HS(n, u):
+            if u == 0:
+                hb[n] = work.tile([P, T, W], BF16, name="hb", bufs=2, align_bytes=64)
+            nc.scalar.activation(out=hb[n][:, u, :], in_=b[n][:, u, :], func=COPY, scale=bloom_f[:, u : u + 1])
+
+        def H(n):
+            hi[n] = grouped("gA")
+            if n in H_ON_SCALAR:
+                interleave("v", hi[n], hb[n], 0, W)
+            else:
+                nc.vector.tensor_tensor(
+                    out=hi[n][:].rearrange("p (c i) t -> p c t i", i=4),
+                    in0=b[n][:].rearrange("p t (c i) -> p c t i", i=4),
+                    in1=bloom_sb[:].unsqueeze(1).unsqueeze(3).to_broadcast([P, W // 4, T, 4]),
+                    op=MULT,
+                )
+
+        def Q_h(n):
+            hq[n] = work.tile([P, W], U32, name="hq", align_bytes=64, bufs=2)
+            hs[n] = work.tile([P, W], U8, name="hs", align_bytes=64, bufs=2)
+            quantize(hq[n], hs[n], hi[n])
+
+        def M3(n, u):
+            ps3[n, u] = psum.tile([P, W], F32, name="y")
+            mm(ps3[n, u], fq, fs, sub(u), hq[n], hs[n], True, True)
+
+        def O(n, u):
+            o = work.tile([P, W], F32, name="o", bufs=6)
+            nc.vector.tensor_tensor(out=o[:], in0=b[n][:, u, :], in1=ps3[n, u][:], op=ADD)
+            nc.sync.dma_start(out=out_v[:, u, cols(n)], in_=o[:])
+
+        with tc.manual_schedule():
+            fraw = raws.tile([P, T, W], BF16, name="raw", align_bytes=64)
+            order = [(g, n) for n in range(G) for g in range(G)]
+            loaded = []
+
+            def loads(k):
+                while len(loaded) < min(k, len(order)):
+                    load_c(*order[len(loaded)])
+                    loaded.append(1)
+
+            def load_vs(g, lo, hi_):
+                nc.sync.dma_start(
+                    out=v_sb[g][:, :, lo:hi_],
+                    in_=v.rearrange("(p t) w -> p t w", t=T)[:, :, g * W + lo : g * W + hi_],
+                )
+
+            nc.scalar.dma_start(out=stay_sb[:], in_=stay.rearrange("(p t) -> p t", t=T))
+            nc.scalar.dma_start(out=bloom_sb[:], in_=bloom.rearrange("(p t) -> p t", t=T))
+            if V_FIRST:
+                load_vs(0, 0, W // 2)
+            nc.sync.dma_start(out=fraw[:], in_=fac.rearrange("(p t) k -> p t k", t=T))
+            if not V_FIRST:
+                load_vs(0, 0, W // 2)
+            load_vs(0, W // 2, W)
+            for g in range(1, G):
+                load_v(g)
+            loads(LOY)
+            nc.sync.dma_start(out=loyal_sb[:], in_=loyal.partition_broadcast(P))
+            loads(8)
+
+            make_identity(nc, ident[:])
+            emitted = {}
+
+            def at(k):
+                for n in range(G):
+                    for g in range(G):
+                        if IC_AT[n][g] == k:
+                            I_c(g, n)
+                            emitted[g, n] = 1
+                for g in range(1, G):
+                    if IV_AT[g] == k:
+                        I_v(g, IV[g])
+                m = 0
+                while m < len(order) and order[m] in emitted:
+                    m += 1
+                loads(8 + m)
+
+            fi = grouped("gA")
+            words = fraw[:].rearrange("p t k -> p (t k)").bitcast(F32)
+            fps = []
+            for h in range(2):
+                ft = psum.tile([P, 2, 2, P], F32, name="y")
+                fps.append(ft)
+                for a in range(2):
+                    for e in range(2):
+                        w0 = (2 * h + a) * (W // 2)
+                        nc.tensor.transpose(ft[:, a, e, :], words[:, w0 + e : w0 + W // 2 : 2], ident[:])
+            fi_words = fi[:].rearrange("p w t -> p (w t)").bitcast(F32).rearrange("p (a m e) -> p a m e", a=T, e=2)
+
+            I_v(0, "s", 0, W // 2)
+            for h in range(2):
+                src = fps[h][:].rearrange("p a e m -> p a m e")
+                dst = fi_words[:, 2 * h : 2 * h + 2]
+                nc.vector.tensor_copy(out=dst, in_=src)
+            I_v(0, "v", W // 2, W)
+            quantize(fq, fs, fi)
+            Q_v(0)
+            nc.vector.tensor_copy(out=bloom_f[:], in_=bloom_sb[:])
+            for u in range(T):
+                M1(0, u)
+            at(0)
+
+            for g in range(G):
+                A(g, 0)
+                A(g, 1)
+                if g + 1 < G:
+                    Q_v(g + 1)
+                    M1(g + 1, 0)
+                    M1(g + 1, 1)
+                TR(g, 0)
+                TR(g, 1)
+                C(g, 0)
+                C(g, 1)
+                at(2 * g + 1)
+                if g > 0:
+                    Q_a(g - 1)
+                A(g, 2)
+                A(g, 3)
+                if g + 1 < G:
+                    M1(g + 1, 2)
+                    M1(g + 1, 3)
+                TR(g, 2)
+                TR(g, 3)
+                C(g, 2)
+                C(g, 3)
+                at(2 * g + 2)
+                if g == D0_AT:
+                    for u in range(T):
+                        D(0, u)
+            for g in range(G):
+                Q_c(g, 0)
+                if g < G - 1:
+                    for u in range(T):
+                        M2(0, u, g)
+            Q_a(G - 1)
+            for u in range(T):
+                M2(0, u, G - 1)
+
+            for n in range(G):
+                last = n == G - 1
+                c0 = 9 + 4 * n
+                at(c0)
+                for u in range(T):
+                    B(n, u)
+                    if not last:
+                        D(n + 1, u)
+                if n in H_ON_SCALAR:
+                    for u in range(T):
+                        HS(n, u)
+                at(c0 + 1)
+                if n > 0:
+                    for u in range(T):
+                        if not (last and u == T - 1):
+                            O(n - 1, u)
+                at(c0 + 2)
+                for g in range(G):
+                    if g == G - 1:
+                        H(n)
+                        if last:
+                            O(n - 1, T - 1)
+                    if not last:
+                        Q_c(g, n + 1)
+                        for u in range(T):
+                            M2(n + 1, u, g)
+                at(c0 + 3)
+                Q_h(n)
+                for u in range(T):
+                    M3(n, u)
+            for u in range(T):
+                O(G - 1, u)

@@ -21,15 +21,16 @@ G = POLLS // W
 FLOPS = 2 * PLANTS * POLLS * (2 * PLANTS + POLLS)
 
 V_FIRST = 0
-H_ON_SCALAR = (0, 3)
-D_V = [0,0,0,0]
+H_ON_SCALAR = (0, 2, 3)
+D_V = [0,1,0,0]
 IV = ["s","s","s","v"]
-IV_AT = [0,0,0,2]
-IC = [["v","v","v","s"],["s","s","s","s"],["s","s","s","s"],["s","s","s","s"]]
-IC_AT = [[4,7,8,4],[9,6,9,10],[12,12,13,12],[15,16,17,18]]
+IV_AT = [0,0,0,1]
+IC = [["v","v","v","s"],["s","s","v","s"],["s","s","s","s"],["s","s","s","s"]]
+IC_AT = [[3,7,4,2],[9,6,9,10],[12,12,13,12],[15,19,17,19]]
 D_BUFS = 1
-D0_AT = 1
-LOY = 3
+D0_AT = 3
+LOY = 4
+QC0_AT = [7,8,8,8]
 
 
 def tile_pollinator_visit_response_t1_kernel(tc, v, fac, comp, stay, loyal, bloom, out):
@@ -51,7 +52,7 @@ def tile_pollinator_visit_response_t1_kernel(tc, v, fac, comp, stay, loyal, bloo
         fs = keep.tile([P, PLANTS], U8, name="fs", align_bytes=64)
         aq = [keep.tile([P, PLANTS], U32, name="aq%d" % g, align_bytes=64) for g in range(G)]
         as_ = [keep.tile([P, PLANTS], U8, name="as%d" % g, align_bytes=64) for g in range(G)]
-        d = {}
+        d = keep.tile([P, T, W], F32, name="d")
 
         out_v = out.rearrange("(p t) w -> p t w", t=T)
         vq, vs, vi, ai, a32, ps1, psT = {}, {}, {}, {}, {}, {}, {}
@@ -120,19 +121,20 @@ def tile_pollinator_visit_response_t1_kernel(tc, v, fac, comp, stay, loyal, bloo
         def A(g, u):
             if u == 0:
                 a32[g] = work.tile([P, T, W], F32, name="w32")
-            nc.vector.scalar_tensor_tensor(
-                out=a32[g][:, u, :].rearrange("p (t m) -> p t m", t=T),
-                in0=v_sb[g][:, u, :].rearrange("p (m t) -> p t m", t=T),
-                scalar=stay_sb[:, u : u + 1],
-                in1=ps1[g, u][:].rearrange("p (m t) -> p t m", t=T),
-                op0=MULT,
-                op1=ADD,
-            )
+            for s in range(2):
+                nc.vector.scalar_tensor_tensor(
+                    out=a32[g][:, u, s * 256 : (s + 1) * 256].rearrange("p (m r) -> p m r", r=2),
+                    in0=v_sb[g][:, u, :].rearrange("p (m t) -> p m t", t=T)[:, :, 2 * s : 2 * s + 2],
+                    scalar=stay_sb[:, u : u + 1],
+                    in1=ps1[g, u][:].rearrange("p (m t) -> p m t", t=T)[:, :, 2 * s : 2 * s + 2],
+                    op0=MULT,
+                    op1=ADD,
+                )
 
         def TR(g, u):
             psT[g, u] = psum.tile([P, T, P], F32, name="y")
             for t in range(T):
-                nc.tensor.transpose(psT[g, u][:, t, :], a32[g][:, u, sub(t)], ident[:])
+                nc.tensor.transpose(psT[g, u][:, t, :], a32[g][:, u, (t // 2) * 256 + t % 2 : (t // 2 + 1) * 256 : 2], ident[:])
 
         def C(g, u):
             if u == 0:
@@ -145,11 +147,10 @@ def tile_pollinator_visit_response_t1_kernel(tc, v, fac, comp, stay, loyal, bloo
             quantize(aq[g], as_[g], ai[g])
 
         def D(g, u):
-            d[g, u] = work.tile([P, W], F32, name="d%d" % u, bufs=D_BUFS)
             (nc.vector if D_V[g] else nc.gpsimd).tensor_tensor(
-                out=d[g, u][:].rearrange("p (m t) -> p m t", t=T),
-                in0=a32[g][:, u, :].rearrange("p (t m) -> p m t", t=T),
-                in1=loyal_sb[:, cols(g)].rearrange("p (m t) -> p m t", t=T),
+                out=d[:, u, :].rearrange("p (m e r) -> p m e r", e=2, r=2),
+                in0=a32[g][:, u, :].rearrange("p (e m r) -> p m e r", e=2, r=2),
+                in1=loyal_sb[:, cols(g)].rearrange("p (m e r) -> p m e r", e=2, r=2),
                 op=MULT,
             )
 
@@ -162,46 +163,75 @@ def tile_pollinator_visit_response_t1_kernel(tc, v, fac, comp, stay, loyal, bloo
             cs[g, n] = work.tile([P, W], U8, name="cs", align_bytes=64, bufs=8)
             quantize(cq[g, n], cs[g, n], ci[g, n])
 
+        HW = W // 2
+
+        def half(h):
+            return slice(h * HW, (h + 1) * HW)
+
+        def mmh(acc, j, lc, ls, u, rc, rs, h, start, stop):
+            nc.tensor.matmul_mx(
+                out=acc[:, j, :],
+                lhsT=lc[:, sub(u)].bitcast(FP8X4),
+                lhsT_scale=ls[:, sub(u)],
+                rhs=rc[:, h].bitcast(FP8X4),
+                rhs_scale=rs[:, h],
+                start=start,
+                stop=stop,
+            )
+
         def M2(n, u, g):
             if g == 0:
                 ps2[n, u] = psum.tile([P, W], F32, name="x")
             mm(ps2[n, u], aq[g], as_[g], sub(u), cq[g, n], cs[g, n], g == 0, g == G - 1)
 
-        def B(n, u):
-            if u == 0:
+        def B(n, u, h, w):
+            if h == 0 and u == 0:
                 b[n] = work.tile([P, T, W], F32, name="w32")
-            nc.vector.tensor_tensor(out=b[n][:, u, :], in0=d[n, u][:], in1=ps2[n, u][:], op=SUB)
+            k = slice(h * HW, h * HW + w)
+            nc.vector.tensor_tensor(out=b[n][:, u, k], in0=d[:, u, k], in1=ps2[n, u][:, k], op=SUB)
 
-        def HS(n, u):
-            if u == 0:
-                hb[n] = work.tile([P, T, W], BF16, name="hb", bufs=2, align_bytes=64)
-            nc.scalar.activation(out=hb[n][:, u, :], in_=b[n][:, u, :], func=COPY, scale=bloom_f[:, u : u + 1])
+        def HS(n, h, w):
+            hb[n, h] = work.tile([P, T, w], BF16, name="hb", bufs=2, align_bytes=64)
+            for u in range(T):
+                nc.scalar.activation(
+                    out=hb[n, h][:, u, :], in_=b[n][:, u, h * HW : h * HW + w], func=COPY, scale=bloom_f[:, u : u + 1]
+                )
 
-        def H(n):
-            hi[n] = grouped("gA")
-            if n in H_ON_SCALAR:
-                interleave("v", hi[n], hb[n], 0, W)
+        def H(n, h, w):
+            hi[n, h] = work.tile([P, w, T], BF16, name="hi", bufs=2, align_bytes=64)
+            if (n, h) in hb:
+                interleave("v", hi[n, h], hb[n, h], 0, w)
             else:
                 nc.vector.tensor_tensor(
-                    out=hi[n][:].rearrange("p (c i) t -> p c t i", i=4),
-                    in0=b[n][:].rearrange("p t (c i) -> p c t i", i=4),
-                    in1=bloom_sb[:].unsqueeze(1).unsqueeze(3).to_broadcast([P, W // 4, T, 4]),
+                    out=hi[n, h][:].rearrange("p (c i) t -> p c t i", i=4),
+                    in0=b[n][:, :, h * HW : h * HW + w].rearrange("p t (c i) -> p c t i", i=4),
+                    in1=bloom_sb[:].unsqueeze(1).unsqueeze(3).to_broadcast([P, w // 4, T, 4]),
                     op=MULT,
                 )
 
-        def Q_h(n):
-            hq[n] = work.tile([P, W], U32, name="hq", align_bytes=64, bufs=2)
-            hs[n] = work.tile([P, W], U8, name="hs", align_bytes=64, bufs=2)
-            quantize(hq[n], hs[n], hi[n])
+        def Q_h(n, h, w):
+            hq[n, h] = work.tile([P, w], U32, name="hq", align_bytes=64, bufs=2)
+            hs[n, h] = work.tile([P, w], U8, name="hs", align_bytes=64, bufs=2)
+            quantize(hq[n, h], hs[n, h], hi[n, h])
 
         def M3(n, u):
             ps3[n, u] = psum.tile([P, W], F32, name="y")
-            mm(ps3[n, u], fq, fs, sub(u), hq[n], hs[n], True, True)
+            mm(ps3[n, u], fq, fs, sub(u), hq[n, 0], hs[n, 0], True, True)
 
         def O(n, u):
             o = work.tile([P, W], F32, name="o", bufs=6)
             nc.vector.tensor_tensor(out=o[:], in0=b[n][:, u, :], in1=ps3[n, u][:], op=ADD)
             nc.sync.dma_start(out=out_v[:, u, cols(n)], in_=o[:])
+
+        def M3h(n, h, q):
+            ps3[n, h, q] = psum.tile([P, 2, HW], F32, name="y")
+            for j in range(2):
+                mmh(ps3[n, h, q], j, fq, fs, 2 * q + j, hq[n, h], hs[n, h], slice(0, HW), True, True)
+
+        def Oh(n, h, q):
+            o = work.tile([P, 2, HW], F32, name="o", bufs=6)
+            nc.vector.tensor_tensor(out=o[:], in0=b[n][:, 2 * q : 2 * q + 2, half(h)], in1=ps3[n, h, q][:], op=ADD)
+            nc.sync.dma_start(out=out_v[:, 2 * q : 2 * q + 2, n * W + h * HW : n * W + (h + 1) * HW], in_=o[:])
 
         with tc.manual_schedule():
             fraw = raws.tile([P, T, W], BF16, name="raw", align_bytes=64)
@@ -245,6 +275,9 @@ def tile_pollinator_visit_response_t1_kernel(tc, v, fac, comp, stay, loyal, bloo
                 for g in range(1, G):
                     if IV_AT[g] == k:
                         I_v(g, IV[g])
+                for g in range(G):
+                    if QC0_AT[g] == k:
+                        Q_c(g, 0)
                 m = 0
                 while m < len(order) and order[m] in emitted:
                     m += 1
@@ -302,44 +335,57 @@ def tile_pollinator_visit_response_t1_kernel(tc, v, fac, comp, stay, loyal, bloo
                 if g == D0_AT:
                     for u in range(T):
                         D(0, u)
-            for g in range(G):
-                Q_c(g, 0)
-                if g < G - 1:
-                    for u in range(T):
-                        M2(0, u, g)
+            for g in range(G - 1):
+                for u in range(T):
+                    M2(0, u, g)
             Q_a(G - 1)
             for u in range(T):
                 M2(0, u, G - 1)
 
-            for n in range(G):
-                last = n == G - 1
+            for n in range(G - 1):
                 c0 = 9 + 4 * n
                 at(c0)
                 for u in range(T):
-                    B(n, u)
-                    if not last:
-                        D(n + 1, u)
+                    B(n, u, 0, W)
                 if n in H_ON_SCALAR:
+                    HS(n, 0, W)
+                if not D_V[n + 1]:
                     for u in range(T):
-                        HS(n, u)
+                        D(n + 1, u)
                 at(c0 + 1)
                 if n > 0:
                     for u in range(T):
-                        if not (last and u == T - 1):
-                            O(n - 1, u)
+                        O(n - 1, u)
                 at(c0 + 2)
                 for g in range(G):
                     if g == G - 1:
-                        H(n)
-                        if last:
-                            O(n - 1, T - 1)
-                    if not last:
-                        Q_c(g, n + 1)
-                        for u in range(T):
-                            M2(n + 1, u, g)
-                at(c0 + 3)
-                Q_h(n)
+                        H(n, 0, W)
+                    Q_c(g, n + 1)
+                    for u in range(T):
+                        M2(n + 1, u, g)
+                    if D_V[n + 1]:
+                        D(n + 1, g)
+                Q_h(n, 0, W)
                 for u in range(T):
                     M3(n, u)
-            for u in range(T):
-                O(G - 1, u)
+                at(c0 + 3)
+            n = G - 1
+            for h in range(2):
+                for u in range(T):
+                    B(n, u, h, HW)
+                if n in H_ON_SCALAR:
+                    HS(n, h, HW)
+                O(n - 1, h)
+            H(n, 0, HW)
+            O(n - 1, 2)
+            Q_h(n, 0, HW)
+            M3h(n, 0, 0)
+            M3h(n, 0, 1)
+            H(n, 1, HW)
+            O(n - 1, 3)
+            Q_h(n, 1, HW)
+            M3h(n, 1, 0)
+            M3h(n, 1, 1)
+            for h in range(2):
+                for q in range(2):
+                    Oh(n, h, q)

@@ -17,375 +17,314 @@ PLANTS, POLLS = 512, 2048
 P = 128
 T = 4
 W = 512
-G = POLLS // W
+BLOCKS = POLLS // W
+RUN = 4
+AHEAD = 8
+
 FLOPS = 2 * PLANTS * POLLS * (2 * PLANTS + POLLS)
 
-V_FIRST = 0
-H_ON_SCALAR = (0, 2, 3)
-D_V = [0,1,0,0]
-IV = ["s","s","s","v"]
-IV_AT = [0,0,0,1]
-IC = [["v","v","v","s"],["s","s","v","s"],["s","s","s","s"],["s","s","s","s"]]
-IC_AT = [[3,7,4,2],[9,6,9,10],[12,12,13,12],[15,19,17,19]]
-D_BUFS = 1
-D0_AT = 3
-LOY = 4
-QC0_AT = [7,8,8,8]
+EARLY_INTERLEAVES = {
+    (1, 0): (("comp", 3, "scalar"), ("v", 3, "vector")),
+    (1, 1): (("comp", 0, "vector"), ("comp", 1, "scalar")),
+    (2, 1): (("comp", 2, "vector"),),
+}
+VECTOR_COMP_TILES = ((2, 1),)
+BLOOM_ON_VECTOR = (1,)
+LOYAL_ON_GPSIMD = (2, 3)
 
 
 def tile_pollinator_visit_response_t1_kernel(tc, v, fac, comp, stay, loyal, bloom, out):
     nc = tc.nc
     with ExitStack() as ctx:
-        const = ctx.enter_context(tc.tile_pool(name="const", bufs=1))
-        raws = ctx.enter_context(tc.tile_pool(name="raws", bufs=9))
         keep = ctx.enter_context(tc.tile_pool(name="keep", bufs=1))
+        loads = ctx.enter_context(tc.tile_pool(name="loads", bufs=AHEAD + 1))
         work = ctx.enter_context(tc.tile_pool(name="work", bufs=4))
         psum = ctx.enter_context(tc.psum_pool(name="psum", bufs=4))
 
-        ident = const.tile([P, P], F32, name="ident")
-        stay_sb = const.tile([P, T], BF16, name="stay_sb")
-        bloom_sb = const.tile([P, T], BF16, name="bloom_sb")
-        bloom_f = const.tile([P, T], F32, name="bloom_f")
-        loyal_sb = const.tile([P, POLLS], BF16, name="loyal_sb")
-        v_sb = [keep.tile([P, T, W], BF16, name="v_sb%d" % g) for g in range(G)]
-        fq = keep.tile([P, PLANTS], U32, name="fq", align_bytes=64)
-        fs = keep.tile([P, PLANTS], U8, name="fs", align_bytes=64)
-        aq = [keep.tile([P, PLANTS], U32, name="aq%d" % g, align_bytes=64) for g in range(G)]
-        as_ = [keep.tile([P, PLANTS], U8, name="as%d" % g, align_bytes=64) for g in range(G)]
+        identity = keep.tile([P, P], F32, name="identity")
+        stay_sb = keep.tile([P, T], BF16, name="stay_sb")
+        bloom_bf16 = keep.tile([P, T], BF16, name="bloom_bf16")
+        bloom_f32 = keep.tile([P, T], F32, name="bloom_f32")
+        loyal_sb = keep.tile([P, POLLS], BF16, name="loyal_sb")
+        v_sb = [keep.tile([P, T, W], BF16, name="v_sb%d" % g) for g in range(BLOCKS)]
+        fac_codes = keep.tile([P, PLANTS], U32, name="fac_codes", align_bytes=64)
+        fac_scales = keep.tile([P, PLANTS], U8, name="fac_scales", align_bytes=64)
+        a_codes = [keep.tile([P, PLANTS], U32, name="a_codes%d" % g, align_bytes=64) for g in range(BLOCKS)]
+        a_scales = [keep.tile([P, PLANTS], U8, name="a_scales%d" % g, align_bytes=64) for g in range(BLOCKS)]
         d = keep.tile([P, T, W], F32, name="d")
 
-        out_v = out.rearrange("(p t) w -> p t w", t=T)
-        vq, vs, vi, ai, a32, ps1, psT = {}, {}, {}, {}, {}, {}, {}
-        raw, ci, cq, cs = {}, {}, {}, {}
-        ps2, b, hb, hi, hq, hs, ps3 = {}, {}, {}, {}, {}, {}, {}
+        v_rows = v.rearrange("(m u) w -> m u w", u=T)
+        fac_rows = fac.rearrange("(m u) k -> m u k", u=T)
+        out_rows = out.rearrange("(m u) w -> m u w", u=T)
 
-        def cols(g):
-            return slice(g * W, (g + 1) * W)
+        v_grouped, v_codes, v_scales, sum1, a, turned, a_grouped = {}, {}, {}, {}, {}, {}, {}
+        comp_sb, comp_grouped, comp_codes, comp_scales, sum2 = {}, {}, {}, {}, {}
+        b, scaled_b, h_grouped, h_codes, h_scales, sum3 = {}, {}, {}, {}, {}, {}
 
-        def sub(u):
+        def block(n):
+            return slice(n * W, (n + 1) * W)
+
+        def slot(u):
             return slice(u * P, (u + 1) * P)
 
-        def load_v(g):
-            nc.sync.dma_start(out=v_sb[g][:], in_=v.rearrange("(p t) w -> p t w", t=T)[:, :, cols(g)])
 
-        def load_c(g, n):
-            raw[g, n] = raws.tile([P, T, W], BF16, name="raw", align_bytes=64)
-            nc.sync.dma_start(
-                out=raw[g, n][:],
-                in_=comp[g * W : (g + 1) * W, cols(n)].rearrange("(p t) w -> p t w", t=T),
-            )
-
-        def grouped(name):
-            return work.tile([P, W, T], BF16, name=name, align_bytes=64)
-
-        def interleave(eng, dst, src, lo, hi_):
-            o = dst[:, lo:hi_, :].rearrange("p (c i) t -> p c t i", i=4)
-            s = src[:, :, lo:hi_].rearrange("p t (c i) -> p c t i", i=4)
-            if eng == "v":
-                nc.vector.tensor_copy(out=o, in_=s)
-            elif eng == "s":
-                nc.scalar.copy(out=o, in_=s)
+        def interleave(engine, grouped, rows, lo, hi):
+            dst = grouped[:, lo:hi, :].rearrange("p (c i) t -> p c t i", i=RUN)
+            src = rows[:, :, lo:hi].rearrange("p t (c i) -> p c t i", i=RUN)
+            if engine == "vector":
+                nc.vector.tensor_copy(out=dst, in_=src)
             else:
-                nc.gpsimd.tensor_scalar(out=o, in0=s, scalar1=1.0, scalar2=0.0, op0=MULT, op1=ADD)
+                nc.scalar.copy(out=dst, in_=src)
 
-        def quantize(codes, scales, src):
+        def quantize(codes, scales, grouped):
             nc.vector.quantize_mx(
-                out=codes[:].bitcast(FP8X4), scales=scales[:], in_=src[:].rearrange("p w t -> p (w t)")
+                out=codes[:].bitcast(FP8X4), scales=scales[:], in_=grouped[:].rearrange("p w t -> p (w t)")
             )
 
-        def mm(acc, lc, ls, lcols, rc, rs, start, stop):
+        def mx_pass(acc, lhs_codes, lhs_scales, u, rhs_codes, rhs_scales, start, stop):
             nc.tensor.matmul_mx(
                 out=acc[:],
-                lhsT=lc[:, lcols].bitcast(FP8X4),
-                lhsT_scale=ls[:, lcols],
-                rhs=rc[:].bitcast(FP8X4),
-                rhs_scale=rs[:],
+                lhsT=lhs_codes[:, slot(u)].bitcast(FP8X4),
+                lhsT_scale=lhs_scales[:, slot(u)],
+                rhs=rhs_codes[:].bitcast(FP8X4),
+                rhs_scale=rhs_scales[:],
                 start=start,
                 stop=stop,
             )
 
-        def I_v(g, eng, lo=0, hi_=W):
-            if g not in vi:
-                vi[g] = grouped("gA")
-            interleave(eng, vi[g], v_sb[g], lo, hi_)
+        def spare_passes(tag):
+            for i in range(2):
+                spare = psum.tile([P, W], F32, name=tag)
+                mx_pass(spare, fac_codes, fac_scales, 0, fac_codes, fac_scales, True, True)
 
-        def Q_v(g):
-            vq[g] = work.tile([P, W], U32, name="vq", align_bytes=64, bufs=2)
-            vs[g] = work.tile([P, W], U8, name="vs", align_bytes=64, bufs=2)
-            quantize(vq[g], vs[g], vi[g])
 
-        def M1(g, u):
-            ps1[g, u] = psum.tile([P, W], F32, name="x")
-            mm(ps1[g, u], fq, fs, sub(u), vq[g], vs[g], True, True)
+        def interleave_v(g, engine, lo=0, hi=W):
+            if g not in v_grouped:
+                v_grouped[g] = work.tile([P, W, T], BF16, name="grouped", align_bytes=64)
+            interleave(engine, v_grouped[g], v_sb[g], lo, hi)
 
-        def A(g, u):
+        def quantize_v(g):
+            v_codes[g] = work.tile([P, W], U32, name="v_codes", align_bytes=64, bufs=2)
+            v_scales[g] = work.tile([P, W], U8, name="v_scales", align_bytes=64, bufs=2)
+            quantize(v_codes[g], v_scales[g], v_grouped[g])
+
+        def product1(g, u):
+            sum1[g, u] = psum.tile([P, W], F32, name="sums")
+            mx_pass(sum1[g, u], fac_codes, fac_scales, u, v_codes[g], v_scales[g], True, True)
+
+        def make_a(g, u):
             if u == 0:
-                a32[g] = work.tile([P, T, W], F32, name="w32")
-            for s in range(2):
+                a[g] = work.tile([P, T, W], F32, name="a")
+            v_words = v_sb[g][:, u, :].rearrange("p (m t) -> p m t", t=T)
+            sum_words = sum1[g, u][:].rearrange("p (m t) -> p m t", t=T)
+            for e in range(2):
+                pair = slice(2 * e, 2 * e + 2)
                 nc.vector.scalar_tensor_tensor(
-                    out=a32[g][:, u, s * 256 : (s + 1) * 256].rearrange("p (m r) -> p m r", r=2),
-                    in0=v_sb[g][:, u, :].rearrange("p (m t) -> p m t", t=T)[:, :, 2 * s : 2 * s + 2],
+                    out=a[g][:, u, e * (W // 2) : (e + 1) * (W // 2)].rearrange("p (m r) -> p m r", r=2),
+                    in0=v_words[:, :, pair],
                     scalar=stay_sb[:, u : u + 1],
-                    in1=ps1[g, u][:].rearrange("p (m t) -> p m t", t=T)[:, :, 2 * s : 2 * s + 2],
+                    in1=sum_words[:, :, pair],
                     op0=MULT,
                     op1=ADD,
                 )
 
-        def TR(g, u):
-            psT[g, u] = psum.tile([P, T, P], F32, name="y")
+        def turn_a(g, u):
+            turned[g, u] = psum.tile([P, T, P], F32, name="turned")
             for t in range(T):
-                nc.tensor.transpose(psT[g, u][:, t, :], a32[g][:, u, (t // 2) * 256 + t % 2 : (t // 2 + 1) * 256 : 2], ident[:])
+                first = (t // 2) * (W // 2) + t % 2
+                last = (t // 2 + 1) * (W // 2)
+                nc.tensor.transpose(turned[g, u][:, t, :], a[g][:, u, first:last:2], identity[:])
 
-        def C(g, u):
+        def round_a(g, u):
             if u == 0:
-                ai[g] = grouped("gA")
-            nc.scalar.copy(
-                out=ai[g][:, sub(u), :], in_=psT[g, u][:].rearrange("p t m -> p m t")
+                a_grouped[g] = work.tile([P, W, T], BF16, name="grouped", align_bytes=64)
+            nc.scalar.copy(out=a_grouped[g][:, slot(u), :], in_=turned[g, u][:].rearrange("p t m -> p m t"))
+
+        def quantize_a(g):
+            quantize(a_codes[g], a_scales[g], a_grouped[g])
+
+
+        def load_comp(g, n):
+            comp_sb[g, n] = loads.tile([P, T, W], BF16, name="loaded", align_bytes=64)
+            nc.sync.dma_start(
+                out=comp_sb[g, n][:], in_=comp[block(g), block(n)].rearrange("(p t) w -> p t w", t=T)
             )
 
-        def Q_a(g):
-            quantize(aq[g], as_[g], ai[g])
+        def interleave_comp(g, n, engine):
+            comp_grouped[g, n] = work.tile([P, W, T], BF16, name="comp_grouped", align_bytes=64, bufs=8)
+            interleave(engine, comp_grouped[g, n], comp_sb[g, n], 0, W)
 
-        def D(g, u):
-            (nc.vector if D_V[g] else nc.gpsimd).tensor_tensor(
+        def quantize_comp(g, n):
+            comp_codes[g, n] = work.tile([P, W], U32, name="comp_codes", align_bytes=64, bufs=8)
+            comp_scales[g, n] = work.tile([P, W], U8, name="comp_scales", align_bytes=64, bufs=8)
+            quantize(comp_codes[g, n], comp_scales[g, n], comp_grouped[g, n])
+
+        def product2(n, g):
+            for u in range(T):
+                if g == 0:
+                    sum2[n, u] = psum.tile([P, W], F32, name="sums")
+                mx_pass(
+                    sum2[n, u], a_codes[g], a_scales[g], u, comp_codes[g, n], comp_scales[g, n],
+                    g == 0, g == BLOCKS - 1,
+                )
+
+        def make_d(n, u):
+            engine = nc.gpsimd if n in LOYAL_ON_GPSIMD else nc.vector
+            engine.tensor_tensor(
                 out=d[:, u, :].rearrange("p (m e r) -> p m e r", e=2, r=2),
-                in0=a32[g][:, u, :].rearrange("p (e m r) -> p m e r", e=2, r=2),
-                in1=loyal_sb[:, cols(g)].rearrange("p (m e r) -> p m e r", e=2, r=2),
+                in0=a[n][:, u, :].rearrange("p (e m r) -> p m e r", e=2, r=2),
+                in1=loyal_sb[:, block(n)].rearrange("p (m e r) -> p m e r", e=2, r=2),
                 op=MULT,
             )
 
-        def I_c(g, n):
-            ci[g, n] = work.tile([P, W, T], BF16, name="ci", align_bytes=64, bufs=8)
-            interleave(IC[n][g], ci[g, n], raw[g, n], 0, W)
+        def make_b(n, u):
+            if u == 0:
+                b[n] = work.tile([P, T, W], F32, name="b", bufs=2)
+            nc.vector.tensor_tensor(out=b[n][:, u, :], in0=d[:, u, :], in1=sum2[n, u][:], op=SUB)
 
-        def Q_c(g, n):
-            cq[g, n] = work.tile([P, W], U32, name="cq", align_bytes=64, bufs=8)
-            cs[g, n] = work.tile([P, W], U8, name="cs", align_bytes=64, bufs=8)
-            quantize(cq[g, n], cs[g, n], ci[g, n])
 
-        HW = W // 2
-
-        def half(h):
-            return slice(h * HW, (h + 1) * HW)
-
-        def mmh(acc, j, lc, ls, u, rc, rs, h, start, stop):
-            nc.tensor.matmul_mx(
-                out=acc[:, j, :],
-                lhsT=lc[:, sub(u)].bitcast(FP8X4),
-                lhsT_scale=ls[:, sub(u)],
-                rhs=rc[:, h].bitcast(FP8X4),
-                rhs_scale=rs[:, h],
-                start=start,
-                stop=stop,
-            )
-
-        def M2(n, u, g):
-            if g == 0:
-                ps2[n, u] = psum.tile([P, W], F32, name="x")
-            mm(ps2[n, u], aq[g], as_[g], sub(u), cq[g, n], cs[g, n], g == 0, g == G - 1)
-
-        def B(n, u, h, w):
-            if h == 0 and u == 0:
-                b[n] = work.tile([P, T, W], F32, name="w32")
-            k = slice(h * HW, h * HW + w)
-            nc.vector.tensor_tensor(out=b[n][:, u, k], in0=d[:, u, k], in1=ps2[n, u][:, k], op=SUB)
-
-        def HS(n, h, w):
-            hb[n, h] = work.tile([P, T, w], BF16, name="hb", bufs=2, align_bytes=64)
+        def scale_b(n):
+            scaled_b[n] = work.tile([P, T, W], BF16, name="scaled_b", bufs=2, align_bytes=64)
             for u in range(T):
                 nc.scalar.activation(
-                    out=hb[n, h][:, u, :], in_=b[n][:, u, h * HW : h * HW + w], func=COPY, scale=bloom_f[:, u : u + 1]
+                    out=scaled_b[n][:, u, :], in_=b[n][:, u, :], func=COPY, scale=bloom_f32[:, u : u + 1]
                 )
 
-        def H(n, h, w):
-            hi[n, h] = work.tile([P, w, T], BF16, name="hi", bufs=2, align_bytes=64)
-            if (n, h) in hb:
-                interleave("v", hi[n, h], hb[n, h], 0, w)
-            else:
+        def make_h(n):
+            h_grouped[n] = work.tile([P, W, T], BF16, name="h_grouped", bufs=2, align_bytes=64)
+            if n in BLOOM_ON_VECTOR:
                 nc.vector.tensor_tensor(
-                    out=hi[n, h][:].rearrange("p (c i) t -> p c t i", i=4),
-                    in0=b[n][:, :, h * HW : h * HW + w].rearrange("p t (c i) -> p c t i", i=4),
-                    in1=bloom_sb[:].unsqueeze(1).unsqueeze(3).to_broadcast([P, w // 4, T, 4]),
+                    out=h_grouped[n][:].rearrange("p (c i) u -> p c u i", i=RUN),
+                    in0=b[n][:].rearrange("p u (c i) -> p c u i", i=RUN),
+                    in1=bloom_bf16[:].unsqueeze(1).unsqueeze(3).to_broadcast([P, W // RUN, T, RUN]),
                     op=MULT,
                 )
+            else:
+                interleave("vector", h_grouped[n], scaled_b[n], 0, W)
 
-        def Q_h(n, h, w):
-            hq[n, h] = work.tile([P, w], U32, name="hq", align_bytes=64, bufs=2)
-            hs[n, h] = work.tile([P, w], U8, name="hs", align_bytes=64, bufs=2)
-            quantize(hq[n, h], hs[n, h], hi[n, h])
+        def quantize_h(n):
+            h_codes[n] = work.tile([P, W], U32, name="h_codes", align_bytes=64, bufs=2)
+            h_scales[n] = work.tile([P, W], U8, name="h_scales", align_bytes=64, bufs=2)
+            quantize(h_codes[n], h_scales[n], h_grouped[n])
 
-        def M3(n, u):
-            ps3[n, u] = psum.tile([P, W], F32, name="y")
-            mm(ps3[n, u], fq, fs, sub(u), hq[n, 0], hs[n, 0], True, True)
+        def product3(n):
+            for u in range(T):
+                sum3[n, u] = psum.tile([P, W], F32, name="turned")
+                mx_pass(sum3[n, u], fac_codes, fac_scales, u, h_codes[n], h_scales[n], True, True)
 
-        def O(n, u):
-            o = work.tile([P, W], F32, name="o", bufs=6)
-            nc.vector.tensor_tensor(out=o[:], in0=b[n][:, u, :], in1=ps3[n, u][:], op=ADD)
-            nc.sync.dma_start(out=out_v[:, u, cols(n)], in_=o[:])
-
-        def M3h(n, h, q):
-            ps3[n, h, q] = psum.tile([P, 2, HW], F32, name="y")
-            for j in range(2):
-                mmh(ps3[n, h, q], j, fq, fs, 2 * q + j, hq[n, h], hs[n, h], slice(0, HW), True, True)
-
-        def Oh(n, h, q):
-            o = work.tile([P, 2, HW], F32, name="o", bufs=6)
-            nc.vector.tensor_tensor(out=o[:], in0=b[n][:, 2 * q : 2 * q + 2, half(h)], in1=ps3[n, h, q][:], op=ADD)
-            nc.sync.dma_start(out=out_v[:, 2 * q : 2 * q + 2, n * W + h * HW : n * W + (h + 1) * HW], in_=o[:])
+        def make_out(n, u):
+            result = work.tile([P, W], F32, name="result", bufs=6)
+            nc.vector.tensor_tensor(out=result[:], in0=b[n][:, u, :], in1=sum3[n, u][:], op=ADD)
+            nc.sync.dma_start(out=out_rows[:, u, block(n)], in_=result[:])
 
         with tc.manual_schedule():
-            fraw = raws.tile([P, T, W], BF16, name="raw", align_bytes=64)
-            order = [(g, n) for n in range(G) for g in range(G)]
-            loaded = []
-
-            def loads(k):
-                while len(loaded) < min(k, len(order)):
-                    load_c(*order[len(loaded)])
-                    loaded.append(1)
-
-            def load_vs(g, lo, hi_):
-                nc.sync.dma_start(
-                    out=v_sb[g][:, :, lo:hi_],
-                    in_=v.rearrange("(p t) w -> p t w", t=T)[:, :, g * W + lo : g * W + hi_],
-                )
-
-            nc.scalar.dma_start(out=stay_sb[:], in_=stay.rearrange("(p t) -> p t", t=T))
-            nc.scalar.dma_start(out=bloom_sb[:], in_=bloom.rearrange("(p t) -> p t", t=T))
-            if V_FIRST:
-                load_vs(0, 0, W // 2)
-            nc.sync.dma_start(out=fraw[:], in_=fac.rearrange("(p t) k -> p t k", t=T))
-            if not V_FIRST:
-                load_vs(0, 0, W // 2)
-            load_vs(0, W // 2, W)
-            for g in range(1, G):
-                load_v(g)
-            loads(LOY)
+            nc.scalar.dma_start(out=stay_sb[:], in_=stay.rearrange("(m u) -> m u", u=T))
+            nc.scalar.dma_start(out=bloom_bf16[:], in_=bloom.rearrange("(m u) -> m u", u=T))
+            fac_sb = loads.tile([P, T, PLANTS], BF16, name="loaded", align_bytes=64)
+            for half in (slice(0, 2), slice(2, 4)):
+                nc.sync.dma_start(out=fac_sb[:, half, :], in_=fac_rows[:, half, :])
+            for half in (slice(0, W // 2), slice(W // 2, W)):
+                nc.sync.dma_start(out=v_sb[0][:, :, half], in_=v_rows[:, :, half])
+            for g in range(1, BLOCKS):
+                nc.sync.dma_start(out=v_sb[g][:], in_=v_rows[:, :, block(g)])
+            for n in range(AHEAD // BLOCKS):
+                for g in range(BLOCKS):
+                    load_comp(g, n)
             nc.sync.dma_start(out=loyal_sb[:], in_=loyal.partition_broadcast(P))
-            loads(8)
 
-            make_identity(nc, ident[:])
-            emitted = {}
+            make_identity(nc, identity[:])
 
-            def at(k):
-                for n in range(G):
-                    for g in range(G):
-                        if IC_AT[n][g] == k:
-                            I_c(g, n)
-                            emitted[g, n] = 1
-                for g in range(1, G):
-                    if IV_AT[g] == k:
-                        I_v(g, IV[g])
-                for g in range(G):
-                    if QC0_AT[g] == k:
-                        Q_c(g, 0)
-                m = 0
-                while m < len(order) and order[m] in emitted:
-                    m += 1
-                loads(8 + m)
-
-            fi = grouped("gA")
-            words = fraw[:].rearrange("p t k -> p (t k)").bitcast(F32)
-            fps = []
-            for h in range(2):
-                ft = psum.tile([P, 2, 2, P], F32, name="y")
-                fps.append(ft)
-                for a in range(2):
+            fac_grouped = work.tile([P, PLANTS, T], BF16, name="grouped", align_bytes=64)
+            fac_words = fac_sb[:].rearrange("p u k -> p (u k)").bitcast(F32)
+            row_words = PLANTS // 2
+            fac_turned = []
+            for half in range(2):
+                bank = psum.tile([P, 2, 2, P], F32, name="turned")
+                fac_turned.append(bank)
+                for j in range(2):
+                    first = (2 * half + j) * row_words
                     for e in range(2):
-                        w0 = (2 * h + a) * (W // 2)
-                        nc.tensor.transpose(ft[:, a, e, :], words[:, w0 + e : w0 + W // 2 : 2], ident[:])
-            fi_words = fi[:].rearrange("p w t -> p (w t)").bitcast(F32).rearrange("p (a m e) -> p a m e", a=T, e=2)
+                        nc.tensor.transpose(
+                            bank[:, j, e, :], fac_words[:, first + e : first + row_words : 2], identity[:]
+                        )
+            grouped_words = fac_grouped[:].rearrange("p w t -> p (w t)").bitcast(F32)
+            grouped_words = grouped_words.rearrange("p (u m e) -> p u m e", u=T, e=2)
 
-            I_v(0, "s", 0, W // 2)
-            for h in range(2):
-                src = fps[h][:].rearrange("p a e m -> p a m e")
-                dst = fi_words[:, 2 * h : 2 * h + 2]
-                nc.vector.tensor_copy(out=dst, in_=src)
-            I_v(0, "v", W // 2, W)
-            quantize(fq, fs, fi)
-            Q_v(0)
-            nc.vector.tensor_copy(out=bloom_f[:], in_=bloom_sb[:])
+            nc.scalar.copy(out=bloom_f32[:], in_=bloom_bf16[:])
+            interleave_v(0, "scalar", 0, W // 2)
+            nc.vector.tensor_copy(out=grouped_words[:, 0:2], in_=fac_turned[0][:].rearrange("p u e m -> p u m e"))
+            nc.scalar.copy(out=grouped_words[:, 2:4], in_=fac_turned[1][:].rearrange("p u e m -> p u m e"))
+            interleave_v(0, "vector", W // 2, W)
+            quantize(fac_codes, fac_scales, fac_grouped)
+            quantize_v(0)
             for u in range(T):
-                M1(0, u)
-            at(0)
+                product1(0, u)
+            interleave_v(1, "scalar")
+            interleave_v(2, "scalar")
 
-            for g in range(G):
-                A(g, 0)
-                A(g, 1)
-                if g + 1 < G:
-                    Q_v(g + 1)
-                    M1(g + 1, 0)
-                    M1(g + 1, 1)
-                TR(g, 0)
-                TR(g, 1)
-                C(g, 0)
-                C(g, 1)
-                at(2 * g + 1)
-                if g > 0:
-                    Q_a(g - 1)
-                A(g, 2)
-                A(g, 3)
-                if g + 1 < G:
-                    M1(g + 1, 2)
-                    M1(g + 1, 3)
-                TR(g, 2)
-                TR(g, 3)
-                C(g, 2)
-                C(g, 3)
-                at(2 * g + 2)
-                if g == D0_AT:
-                    for u in range(T):
-                        D(0, u)
-            for g in range(G - 1):
-                for u in range(T):
-                    M2(0, u, g)
-            Q_a(G - 1)
+            for g in range(BLOCKS):
+                for q in range(2):
+                    pair = (2 * q, 2 * q + 1)
+                    for u in pair:
+                        make_a(g, u)
+                    if g + 1 < BLOCKS:
+                        if q == 0:
+                            quantize_v(g + 1)
+                        for u in pair:
+                            product1(g + 1, u)
+                    for u in pair:
+                        turn_a(g, u)
+                    for u in pair:
+                        round_a(g, u)
+                    for operand, k, engine in EARLY_INTERLEAVES.get((g, q), ()):
+                        if operand == "v":
+                            interleave_v(k, engine)
+                        else:
+                            interleave_comp(k, 0, engine)
+                    if q == 0 and g > 0:
+                        quantize_a(g - 1)
+
+            for g in range(BLOCKS):
+                load_comp(g, 2)
+                quantize_comp(g, 0)
+            for g in range(BLOCKS - 1):
+                product2(0, g)
+            quantize_a(BLOCKS - 1)
             for u in range(T):
-                M2(0, u, G - 1)
+                make_d(0, u)
+            product2(0, BLOCKS - 1)
 
-            for n in range(G - 1):
-                c0 = 9 + 4 * n
-                at(c0)
+            for n in range(BLOCKS):
+                more = n + 1 < BLOCKS
+                if more:
+                    for g in range(BLOCKS):
+                        interleave_comp(g, n + 1, "vector" if (g, n + 1) in VECTOR_COMP_TILES else "scalar")
+                    if n == 0:
+                        for g in range(BLOCKS):
+                            load_comp(g, 3)
                 for u in range(T):
-                    B(n, u, 0, W)
-                if n in H_ON_SCALAR:
-                    HS(n, 0, W)
-                if not D_V[n + 1]:
+                    make_b(n, u)
+                    if u == 1:
+                        spare_passes("sums")
+                if n not in BLOOM_ON_VECTOR:
+                    scale_b(n)
+                if more and n + 1 in LOYAL_ON_GPSIMD:
                     for u in range(T):
-                        D(n + 1, u)
-                at(c0 + 1)
+                        make_d(n + 1, u)
                 if n > 0:
                     for u in range(T):
-                        O(n - 1, u)
-                at(c0 + 2)
-                for g in range(G):
-                    if g == G - 1:
-                        H(n, 0, W)
-                    Q_c(g, n + 1)
-                    for u in range(T):
-                        M2(n + 1, u, g)
-                    if D_V[n + 1]:
-                        D(n + 1, g)
-                Q_h(n, 0, W)
-                for u in range(T):
-                    M3(n, u)
-                at(c0 + 3)
-            n = G - 1
-            for h in range(2):
-                for u in range(T):
-                    B(n, u, h, HW)
-                if n in H_ON_SCALAR:
-                    HS(n, h, HW)
-                O(n - 1, h)
-            H(n, 0, HW)
-            O(n - 1, 2)
-            Q_h(n, 0, HW)
-            M3h(n, 0, 0)
-            M3h(n, 0, 1)
-            H(n, 1, HW)
-            O(n - 1, 3)
-            Q_h(n, 1, HW)
-            M3h(n, 1, 0)
-            M3h(n, 1, 1)
-            for h in range(2):
-                for q in range(2):
-                    Oh(n, h, q)
+                        make_out(n - 1, u)
+                        if u % 2 == 1:
+                            spare_passes("turned")
+                for g in range(BLOCKS):
+                    if g == BLOCKS - 1:
+                        make_h(n)
+                    if more:
+                        quantize_comp(g, n + 1)
+                        product2(n + 1, g)
+                        if n + 1 not in LOYAL_ON_GPSIMD:
+                            make_d(n + 1, g)
+                quantize_h(n)
+                product3(n)
+            for u in range(T):
+                make_out(BLOCKS - 1, u)

from contextlib import ExitStack

import concourse.mybir as mybir
from concourse.masks import make_identity

F32 = mybir.dt.float32
BF16 = mybir.dt.bfloat16
U32 = mybir.dt.uint32
U8 = mybir.dt.uint8
FP8X4 = mybir.dt.float8_e4m3fn_x4
ADD = mybir.AluOpType.add
SUB = mybir.AluOpType.subtract
MULT = mybir.AluOpType.mult
COPY = mybir.ActivationFunctionType.Copy

PLANTS, POLLS = 512, 2048
P = 128
T = 4
W = 512
BLOCKS = POLLS // W
RUN = 4
AHEAD = 8

FLOPS = 2 * PLANTS * POLLS * (2 * PLANTS + POLLS)

EARLY_INTERLEAVES = {
    (1, 0): (("comp", 3, "scalar"), ("v", 3, "vector")),
    (1, 1): (("comp", 0, "vector"), ("comp", 1, "scalar")),
    (2, 1): (("comp", 2, "vector"),),
}
VECTOR_COMP_TILES = ((2, 1),)
BLOOM_ON_VECTOR = (1,)
LOYAL_ON_GPSIMD = (2, 3)


def tile_pollinator_visit_response_t1_kernel(tc, v, fac, comp, stay, loyal, bloom, out):
    nc = tc.nc
    with ExitStack() as ctx:
        keep = ctx.enter_context(tc.tile_pool(name="keep", bufs=1))
        loads = ctx.enter_context(tc.tile_pool(name="loads", bufs=AHEAD + 1))
        work = ctx.enter_context(tc.tile_pool(name="work", bufs=4))
        psum = ctx.enter_context(tc.psum_pool(name="psum", bufs=4))

        identity = keep.tile([P, P], F32, name="identity")
        stay_sb = keep.tile([P, T], BF16, name="stay_sb")
        bloom_bf16 = keep.tile([P, T], BF16, name="bloom_bf16")
        bloom_f32 = keep.tile([P, T], F32, name="bloom_f32")
        loyal_sb = keep.tile([P, POLLS], BF16, name="loyal_sb")
        v_sb = [keep.tile([P, T, W], BF16, name="v_sb%d" % g) for g in range(BLOCKS)]
        fac_codes = keep.tile([P, PLANTS], U32, name="fac_codes", align_bytes=64)
        fac_scales = keep.tile([P, PLANTS], U8, name="fac_scales", align_bytes=64)
        a_codes = [keep.tile([P, PLANTS], U32, name="a_codes%d" % g, align_bytes=64) for g in range(BLOCKS)]
        a_scales = [keep.tile([P, PLANTS], U8, name="a_scales%d" % g, align_bytes=64) for g in range(BLOCKS)]
        d = keep.tile([P, T, W], F32, name="d")

        v_rows = v.rearrange("(m u) w -> m u w", u=T)
        fac_rows = fac.rearrange("(m u) k -> m u k", u=T)
        out_rows = out.rearrange("(m u) w -> m u w", u=T)

        v_grouped, v_codes, v_scales, sum1, a, turned, a_grouped = {}, {}, {}, {}, {}, {}, {}
        comp_sb, comp_grouped, comp_codes, comp_scales, sum2 = {}, {}, {}, {}, {}
        b, scaled_b, h_grouped, h_codes, h_scales, sum3 = {}, {}, {}, {}, {}, {}

        def block(n):
            return slice(n * W, (n + 1) * W)

        def slot(u):
            return slice(u * P, (u + 1) * P)


        def interleave(engine, grouped, rows, lo, hi):
            dst = grouped[:, lo:hi, :].rearrange("p (c i) t -> p c t i", i=RUN)
            src = rows[:, :, lo:hi].rearrange("p t (c i) -> p c t i", i=RUN)
            if engine == "vector":
                nc.vector.tensor_copy(out=dst, in_=src)
            else:
                nc.scalar.copy(out=dst, in_=src)

        def quantize(codes, scales, grouped):
            nc.vector.quantize_mx(
                out=codes[:].bitcast(FP8X4), scales=scales[:], in_=grouped[:].rearrange("p w t -> p (w t)")
            )

        def mx_pass(acc, lhs_codes, lhs_scales, u, rhs_codes, rhs_scales, start, stop):
            nc.tensor.matmul_mx(
                out=acc[:],
                lhsT=lhs_codes[:, slot(u)].bitcast(FP8X4),
                lhsT_scale=lhs_scales[:, slot(u)],
                rhs=rhs_codes[:].bitcast(FP8X4),
                rhs_scale=rhs_scales[:],
                start=start,
                stop=stop,
            )

        def spare_passes(tag):
            for i in range(2):
                spare = psum.tile([P, W], F32, name=tag)
                mx_pass(spare, fac_codes, fac_scales, 0, fac_codes, fac_scales, True, True)


        def interleave_v(g, engine, lo=0, hi=W):
            if g not in v_grouped:
                v_grouped[g] = work.tile([P, W, T], BF16, name="grouped", align_bytes=64)
            interleave(engine, v_grouped[g], v_sb[g], lo, hi)

        def quantize_v(g):
            v_codes[g] = work.tile([P, W], U32, name="v_codes", align_bytes=64, bufs=2)
            v_scales[g] = work.tile([P, W], U8, name="v_scales", align_bytes=64, bufs=2)
            quantize(v_codes[g], v_scales[g], v_grouped[g])

        def product1(g, u):
            sum1[g, u] = psum.tile([P, W], F32, name="sums")
            mx_pass(sum1[g, u], fac_codes, fac_scales, u, v_codes[g], v_scales[g], True, True)

        def make_a(g, u):
            if u == 0:
                a[g] = work.tile([P, T, W], F32, name="a")
            v_words = v_sb[g][:, u, :].rearrange("p (m t) -> p m t", t=T)
            sum_words = sum1[g, u][:].rearrange("p (m t) -> p m t", t=T)
            for e in range(2):
                pair = slice(2 * e, 2 * e + 2)
                nc.vector.scalar_tensor_tensor(
                    out=a[g][:, u, e * (W // 2) : (e + 1) * (W // 2)].rearrange("p (m r) -> p m r", r=2),
                    in0=v_words[:, :, pair],
                    scalar=stay_sb[:, u : u + 1],
                    in1=sum_words[:, :, pair],
                    op0=MULT,
                    op1=ADD,
                )

        def turn_a(g, u):
            turned[g, u] = psum.tile([P, T, P], F32, name="turned")
            for t in range(T):
                first = (t // 2) * (W // 2) + t % 2
                last = (t // 2 + 1) * (W // 2)
                nc.tensor.transpose(turned[g, u][:, t, :], a[g][:, u, first:last:2], identity[:])

        def round_a(g, u):
            if u == 0:
                a_grouped[g] = work.tile([P, W, T], BF16, name="grouped", align_bytes=64)
            nc.scalar.copy(out=a_grouped[g][:, slot(u), :], in_=turned[g, u][:].rearrange("p t m -> p m t"))

        def quantize_a(g):
            quantize(a_codes[g], a_scales[g], a_grouped[g])


        def load_comp(g, n):
            comp_sb[g, n] = loads.tile([P, T, W], BF16, name="loaded", align_bytes=64)
            nc.sync.dma_start(
                out=comp_sb[g, n][:], in_=comp[block(g), block(n)].rearrange("(p t) w -> p t w", t=T)
            )

        def interleave_comp(g, n, engine):
            comp_grouped[g, n] = work.tile([P, W, T], BF16, name="comp_grouped", align_bytes=64, bufs=8)
            interleave(engine, comp_grouped[g, n], comp_sb[g, n], 0, W)

        def quantize_comp(g, n):
            comp_codes[g, n] = work.tile([P, W], U32, name="comp_codes", align_bytes=64, bufs=8)
            comp_scales[g, n] = work.tile([P, W], U8, name="comp_scales", align_bytes=64, bufs=8)
            quantize(comp_codes[g, n], comp_scales[g, n], comp_grouped[g, n])

        def product2(n, g):
            for u in range(T):
                if g == 0:
                    sum2[n, u] = psum.tile([P, W], F32, name="sums")
                mx_pass(
                    sum2[n, u], a_codes[g], a_scales[g], u, comp_codes[g, n], comp_scales[g, n],
                    g == 0, g == BLOCKS - 1,
                )

        def make_d(n, u):
            engine = nc.gpsimd if n in LOYAL_ON_GPSIMD else nc.vector
            engine.tensor_tensor(
                out=d[:, u, :].rearrange("p (m e r) -> p m e r", e=2, r=2),
                in0=a[n][:, u, :].rearrange("p (e m r) -> p m e r", e=2, r=2),
                in1=loyal_sb[:, block(n)].rearrange("p (m e r) -> p m e r", e=2, r=2),
                op=MULT,
            )

        def make_b(n, u):
            if u == 0:
                b[n] = work.tile([P, T, W], F32, name="b", bufs=2)
            nc.vector.tensor_tensor(out=b[n][:, u, :], in0=d[:, u, :], in1=sum2[n, u][:], op=SUB)


        def scale_b(n):
            scaled_b[n] = work.tile([P, T, W], BF16, name="scaled_b", bufs=2, align_bytes=64)
            for u in range(T):
                nc.scalar.activation(
                    out=scaled_b[n][:, u, :], in_=b[n][:, u, :], func=COPY, scale=bloom_f32[:, u : u + 1]
                )

        def make_h(n):
            h_grouped[n] = work.tile([P, W, T], BF16, name="h_grouped", bufs=2, align_bytes=64)
            if n in BLOOM_ON_VECTOR:
                nc.vector.tensor_tensor(
                    out=h_grouped[n][:].rearrange("p (c i) u -> p c u i", i=RUN),
                    in0=b[n][:].rearrange("p u (c i) -> p c u i", i=RUN),
                    in1=bloom_bf16[:].unsqueeze(1).unsqueeze(3).to_broadcast([P, W // RUN, T, RUN]),
                    op=MULT,
                )
            else:
                interleave("vector", h_grouped[n], scaled_b[n], 0, W)

        def quantize_h(n):
            h_codes[n] = work.tile([P, W], U32, name="h_codes", align_bytes=64, bufs=2)
            h_scales[n] = work.tile([P, W], U8, name="h_scales", align_bytes=64, bufs=2)
            quantize(h_codes[n], h_scales[n], h_grouped[n])

        def product3(n):
            for u in range(T):
                sum3[n, u] = psum.tile([P, W], F32, name="turned")
                mx_pass(sum3[n, u], fac_codes, fac_scales, u, h_codes[n], h_scales[n], True, True)

        def make_out(n, u):
            result = work.tile([P, W], F32, name="result", bufs=6)
            nc.vector.tensor_tensor(out=result[:], in0=b[n][:, u, :], in1=sum3[n, u][:], op=ADD)
            nc.sync.dma_start(out=out_rows[:, u, block(n)], in_=result[:])

        with tc.manual_schedule():
            nc.scalar.dma_start(out=stay_sb[:], in_=stay.rearrange("(m u) -> m u", u=T))
            nc.scalar.dma_start(out=bloom_bf16[:], in_=bloom.rearrange("(m u) -> m u", u=T))
            fac_sb = loads.tile([P, T, PLANTS], BF16, name="loaded", align_bytes=64)
            for half in (slice(0, 2), slice(2, 4)):
                nc.sync.dma_start(out=fac_sb[:, half, :], in_=fac_rows[:, half, :])
            for half in (slice(0, W // 2), slice(W // 2, W)):
                nc.sync.dma_start(out=v_sb[0][:, :, half], in_=v_rows[:, :, half])
            for g in range(1, BLOCKS):
                nc.sync.dma_start(out=v_sb[g][:], in_=v_rows[:, :, block(g)])
            for n in range(AHEAD // BLOCKS):
                for g in range(BLOCKS):
                    load_comp(g, n)
            nc.sync.dma_start(out=loyal_sb[:], in_=loyal.partition_broadcast(P))

            make_identity(nc, identity[:])

            fac_grouped = work.tile([P, PLANTS, T], BF16, name="grouped", align_bytes=64)
            fac_words = fac_sb[:].rearrange("p u k -> p (u k)").bitcast(F32)
            row_words = PLANTS // 2
            fac_turned = []
            for half in range(2):
                bank = psum.tile([P, 2, 2, P], F32, name="turned")
                fac_turned.append(bank)
                for j in range(2):
                    first = (2 * half + j) * row_words
                    for e in range(2):
                        nc.tensor.transpose(
                            bank[:, j, e, :], fac_words[:, first + e : first + row_words : 2], identity[:]
                        )
            grouped_words = fac_grouped[:].rearrange("p w t -> p (w t)").bitcast(F32)
            grouped_words = grouped_words.rearrange("p (u m e) -> p u m e", u=T, e=2)

            nc.scalar.copy(out=bloom_f32[:], in_=bloom_bf16[:])
            interleave_v(0, "scalar", 0, W // 2)
            nc.vector.tensor_copy(out=grouped_words[:, 0:2], in_=fac_turned[0][:].rearrange("p u e m -> p u m e"))
            nc.scalar.copy(out=grouped_words[:, 2:4], in_=fac_turned[1][:].rearrange("p u e m -> p u m e"))
            interleave_v(0, "vector", W // 2, W)
            quantize(fac_codes, fac_scales, fac_grouped)
            quantize_v(0)
            for u in range(T):
                product1(0, u)
            interleave_v(1, "scalar")
            interleave_v(2, "scalar")

            for g in range(BLOCKS):
                for q in range(2):
                    pair = (2 * q, 2 * q + 1)
                    for u in pair:
                        make_a(g, u)
                    if g + 1 < BLOCKS:
                        if q == 0:
                            quantize_v(g + 1)
                        for u in pair:
                            product1(g + 1, u)
                    for u in pair:
                        turn_a(g, u)
                    for u in pair:
                        round_a(g, u)
                    for operand, k, engine in EARLY_INTERLEAVES.get((g, q), ()):
                        if operand == "v":
                            interleave_v(k, engine)
                        else:
                            interleave_comp(k, 0, engine)
                    if q == 0 and g > 0:
                        quantize_a(g - 1)

            for g in range(BLOCKS):
                load_comp(g, 2)
                quantize_comp(g, 0)
            for g in range(BLOCKS - 1):
                product2(0, g)
            quantize_a(BLOCKS - 1)
            for u in range(T):
                make_d(0, u)
            product2(0, BLOCKS - 1)

            for n in range(BLOCKS):
                more = n + 1 < BLOCKS
                if more:
                    for g in range(BLOCKS):
                        interleave_comp(g, n + 1, "vector" if (g, n + 1) in VECTOR_COMP_TILES else "scalar")
                    if n == 0:
                        for g in range(BLOCKS):
                            load_comp(g, 3)
                for u in range(T):
                    make_b(n, u)
                    if u == 1:
                        spare_passes("sums")
                if n not in BLOOM_ON_VECTOR:
                    scale_b(n)
                if more and n + 1 in LOYAL_ON_GPSIMD:
                    for u in range(T):
                        make_d(n + 1, u)
                if n > 0:
                    for u in range(T):
                        make_out(n - 1, u)
                        if u % 2 == 1:
                            spare_passes("turned")
                for g in range(BLOCKS):
                    if g == BLOCKS - 1:
                        make_h(n)
                    if more:
                        quantize_comp(g, n + 1)
                        product2(n + 1, g)
                        if n + 1 not in LOYAL_ON_GPSIMD:
                            make_d(n + 1, g)
                quantize_h(n)
                product3(n)
            for u in range(T):
                make_out(BLOCKS - 1, u)
